import numpy as np
import ml_dtypes


def mxq(x, axis, fmt="e4m3"):
    dtype, down = {"e4m3": (ml_dtypes.float8_e4m3fn, 7), "e5m2": (ml_dtypes.float8_e5m2, 14)}[fmt]
    v = np.moveaxis(np.asarray(x, np.float32).astype(ml_dtypes.bfloat16).astype(np.float64), axis, -1)
    blocks = v.reshape(v.shape[:-1] + (-1, 32))
    amax = np.abs(blocks).max(-1, keepdims=True)
    byte = np.maximum(np.where(amax > 0, np.frexp(amax)[1] - 1 + 127, 0) - down, 1)
    scale = np.exp2(byte - 127.0)
    codes = (blocks / scale).astype(np.float32).astype(dtype).astype(np.float64)
    return np.moveaxis((codes * scale).reshape(v.shape), -1, axis)


WIDE = False


def mx_kscale(k):
    if not WIDE:
        return np.ones(k)
    levels = np.array([10, -10, 5, -5, 0])
    if k % 512:
        return np.exp2(np.random.permutation(np.resize(levels, k // 32))).repeat(32)
    a = np.empty((k // 512, 16))
    for p in range(k // 512):
        a[p, :8] = np.random.permutation(np.resize(levels, 8))
        for g in range(8):
            far = levels[np.abs(levels - a[p, g]) >= 10]
            a[p, g + 8] = far[np.random.randint(len(far))]
    return np.exp2(a.ravel()).repeat(32)


def f64(x):
    return np.asarray(x).astype(np.float64)


def striped(idx):
    return np.tile(np.asarray(idx).reshape(-1, 16).T, (8, 1)).astype(np.uint16)


def unstriped(offs):
    return offs[:16].T.reshape(-1).astype(np.int64)


B, N, T, D, DV, NQ = 1, 512, 1024, 512, 256, 256


def setup_inputs():
    n = np.random.standard_normal
    idx = np.random.permutation(T)[:B * N]
    s = mx_kscale(D)[:, None]
    u = np.ones(T)
    u[idx] = mx_kscale(B * N)
    r = np.random.uniform(0.5, 2.0, T)
    qidx = np.random.permutation(T)[:B * NQ]
    k = n((D, T)) / s
    v = n((DV, T)) / (u * r)
    return {
        "xq": (n((D, T)) * s * (0.60 / np.sqrt(D))).astype(np.float32),
        "kT": k.astype(np.float32),
        "vT": v.astype(np.float32),
        "vs": np.tile(u * r, (128, 1)).astype(np.float32),
        "sink": (2.0 + 3.0 * n((B, NQ, 1))).astype(np.float32),
        "offs": striped(idx),
        "qoffs": striped(qidx),
    }


def reference(xq, kT, vT, vs, sink, offs, qoffs):
    idx = unstriped(offs)
    k = f64(kT)
    v = f64(vT)
    pick = lambda x: x[:, idx].reshape(x.shape[0], B, N).transpose(1, 0, 2)
    q = f64(xq)[:, unstriped(qoffs)].reshape(D, B, NQ).transpose(1, 0, 2)
    score = mxq(q, 1, "e4m3").transpose(0, 2, 1) @ mxq(pick(k), 1, "e4m3")
    m = np.maximum(score.max(-1, keepdims=True), f64(sink))
    p = np.exp(score - m)
    total = p.sum(-1, keepdims=True) + np.exp(f64(sink) - m)
    w = p * pick(f64(vs))[:, :1, :]
    y = mxq(w, 2, "e4m3") @ mxq(pick(v).transpose(0, 2, 1), 1, "e4m3")
    y = y / total
    out = np.zeros((DV, T))
    out[:, unstriped(qoffs)] = y.transpose(2, 0, 1).reshape(-1, B * NQ)
    return out

@@ -1,0 +1,198 @@
+from contextlib import ExitStack
+
+import concourse.mybir as mybir
+from concourse.masks import make_identity
+
+D, T, N, NQ, DV = 512, 1024, 512, 256, 256
+P = 128
+FLOPS = 2 * NQ * N * D + 2 * NQ * N * DV
+
+F32 = mybir.dt.float32
+BF16 = mybir.dt.bfloat16
+U32 = mybir.dt.uint32
+U16 = mybir.dt.uint16
+U8 = mybir.dt.uint8
+FP8X4 = mybir.dt.float8_e4m3fn_x4
+
+COPY = mybir.ActivationFunctionType.Copy
+EXP = mybir.ActivationFunctionType.Exp
+MULT = mybir.AluOpType.mult
+ADD = mybir.AluOpType.add
+X = mybir.AxisListType.X
+
+K_SPLIT = 384
+V_SPLIT = T
+MIN = mybir.AluOpType.min
+
+
+def tile_attend_x_router_sink_kernel(tc, xq, kT, vT, vs, sink, offs, qoffs, out):
+    nc = tc.nc
+    with ExitStack() as ctx:
+        keep = ctx.enter_context(tc.tile_pool(name="keep", bufs=1))
+        ps = ctx.enter_context(tc.psum_pool(name="ps", bufs=2))
+
+        offs_t = keep.tile([P, N // 16], U16, name="offs_t")
+        qoffs_t = keep.tile([P, NQ // 16], U16, name="qoffs_t")
+        vs_raw = keep.tile([P, T], F32, name="vs_raw")
+        k_raw = [keep.tile([P, 2, T], F32, name=f"k_raw{h}") for h in range(2)]
+        v_raw = keep.tile([P, 2, T], F32, name="v_raw")
+        q_raw = [keep.tile([P, T], F32, name=f"q_raw{j}") for j in range(4)]
+        k_rows = kT.rearrange("(p j) n -> p j n", j=4)
+        q_rows = xq.rearrange("(p j) n -> p j n", j=4)
+
+        nc.sync.dma_start(offs_t[:], offs)
+        nc.sync.dma_start(out=vs_raw[:], in_=vs)
+        for h in range(2):
+            nc.sync.dma_start(out=k_raw[h][:], in_=k_rows[:, 2 * h : 2 * h + 2, :])
+        nc.sync.dma_start(qoffs_t[:], qoffs)
+        nc.sync.dma_start(out=v_raw[:], in_=vT.rearrange("(p h) n -> p h n", h=2))
+        for j in range(4):
+            nc.sync.dma_start(out=q_raw[j][:], in_=q_rows[:, j, :])
+
+        ident_f = keep.tile([P, P], F32, name="ident_f")
+        make_identity(nc, ident_f[:])
+        sink_row = keep.tile([P, NQ], F32, name="sink_row")
+        nc.gpsimd.memset(sink_row[:], 0.0)
+        nc.scalar.dma_start(out=sink_row[0:1, :], in_=sink.rearrange("b q o -> b (q o)"))
+        ident_b = keep.tile([P, P], BF16, name="ident_b")
+        make_identity(nc, ident_b[:])
+        placed = [keep.tile([P, T], F32, name=f"placed{h}") for h in range(2)]
+        for h in range(2):
+            nc.gpsimd.memset(placed[h][:], 0.0)
+        dummy = keep.tile([P, 1], F32, name="dummy")
+        nc.scalar.activation(out=dummy[:], in_=ident_f[:, 0:1], func=EXP)
+
+        vs_g = keep.tile([P, N], F32, name="vs_g")
+        nc.vector.tensor_copy(vs_g[:], vs_raw[:].indirect(offs_t[:]))
+        vs_ps = ps.tile([P, 4, P], F32, name="vs_ps", tag="turn")
+        for t in range(4):
+            nc.tensor.transpose(vs_ps[:, t, :], vs_g[:, t::4], ident_f[:])
+        vs_c = keep.tile([P, 4], F32, name="vs_c")
+        nc.scalar.activation(out=vs_c[:], in_=vs_ps[:, :, 0], func=COPY)
+
+        sink_ps = ps.tile([P, 2, P], F32, name="sink_ps", tag="y")
+        for c in range(2):
+            nc.tensor.transpose(sink_ps[:, c, :], sink_row[:, c * P : (c + 1) * P], ident_f[:])
+        sink_n = keep.tile([P, 2], F32, name="sink_n")
+        nc.scalar.activation(out=sink_n[:], in_=sink_ps[:, :, 0], func=COPY, scale=-1.0)
+
+        def cast_pairs(dst, raw, split):
+            nc.scalar.activation(out=dst[:, :split, :], in_=raw[:, :, :split].rearrange("p u n -> p n u"), func=COPY)
+            if split < T:
+                nc.vector.tensor_copy(out=dst[:, split:, :], in_=raw[:, :, split:].rearrange("p u n -> p n u"))
+
+        k_g = keep.tile([P, N * 4], BF16, name="k_g", align_bytes=64)
+        k_words = k_g[:].bitcast(U32).rearrange("p (t s u) -> p s t u", t=4, u=2)
+        for h in range(2):
+            k_pair = keep.tile([P, T, 2], BF16, name=f"k_pair{h}")
+            cast_pairs(k_pair, k_raw[h], K_SPLIT)
+            window = k_pair[:].rearrange("p n u -> p (n u)").bitcast(U32)
+            nc.vector.tensor_copy(k_words[:, :, :, h], window.indirect(offs_t[:]))
+        k_codes = keep.tile([P, N], U32, name="k_codes", align_bytes=64)
+        k_scales = keep.tile([P, N], U8, name="k_scales", align_bytes=64)
+        nc.vector.quantize_mx(out=k_codes[:].bitcast(FP8X4), scales=k_scales[:], in_=k_g[:])
+
+        v_pair = keep.tile([P, T, 2], BF16, name="v_pair")
+        cast_pairs(v_pair, v_raw, V_SPLIT)
+        v_g = keep.tile([P, N, 2], BF16, name="v_g")
+        v_words = v_g[:].rearrange("p n u -> p (n u)").bitcast(U32).rearrange("p (t s) -> p s t", t=4)
+        window = v_pair[:].rearrange("p n u -> p (n u)").bitcast(U32)
+        nc.vector.tensor_copy(v_words, window.indirect(offs_t[:]))
+        v_ps = ps.tile([P, 4, 2, P], BF16, name="v_ps", tag="turn")
+        for t in range(4):
+            for h in range(2):
+                nc.tensor.transpose(v_ps[:, t, h, :], v_g[:, t * P : (t + 1) * P, h], ident_b[:])
+        v_s = keep.tile([P, 2 * P, 4], BF16, name="v_s", align_bytes=64)
+        nc.scalar.copy(out=v_s[:], in_=v_ps[:].rearrange("s t h e -> s (h e) t"))
+        v_codes = keep.tile([P, DV], U32, name="v_codes", align_bytes=64)
+        v_scales = keep.tile([P, DV], U8, name="v_scales", align_bytes=64)
+        nc.vector.quantize_mx(out=v_codes[:].bitcast(FP8X4), scales=v_scales[:], in_=v_s[:].rearrange("p e t -> p (e t)"))
+
+        q_g = keep.tile([P, NQ, 4], BF16, name="q_g", align_bytes=64)
+        for j in range(4):
+            nc.vector.tensor_copy(q_g[:, :, j], q_raw[j][:].indirect(qoffs_t[:]))
+        q_codes = keep.tile([P, NQ], U32, name="q_codes", align_bytes=64)
+        q_scales = keep.tile([P, NQ], U8, name="q_scales", align_bytes=64)
+        for c in range(2):
+            cols = slice(c * P, (c + 1) * P)
+            nc.vector.quantize_mx(
+                out=q_codes[:, cols].bitcast(FP8X4), scales=q_scales[:, cols], in_=q_g[:, cols, :].rearrange("p q j -> p (q j)")
+            )
+
+        scores, probs, sums = [], [], []
+        recip_b = [keep.tile([P, P], F32, name=f"recip_b{c}") for c in range(2)]
+        for c in range(2):
+            cols = slice(c * P, (c + 1) * P)
+            sc = ps.tile([P, N], F32, name="sc", tag="score")
+            nc.tensor.matmul_mx(
+                out=sc[:],
+                lhsT=q_codes[:, cols].bitcast(FP8X4),
+                lhsT_scale=q_scales[:, cols],
+                rhs=k_codes[:].bitcast(FP8X4),
+                rhs_scale=k_scales[:],
+                start=True,
+                stop=True,
+            )
+            scores.append(sc)
+        negm, y_banks = [], []
+        for c in range(2):
+            nm = keep.tile([P, 1], F32, name=f"negm{c}")
+            flipped = keep.tile([P, N], F32, name=f"flipped{c}")
+            nc.vector.tensor_scalar(
+                out=flipped[:], in0=scores[c][:], scalar1=-1.0, scalar2=sink_n[:, c : c + 1], op0=MULT, op1=MIN, accum_out=nm[:]
+            )
+            negm.append(nm)
+        for c in range(2):
+            p = keep.tile([P, N], F32, name=f"p{c}")
+            total = keep.tile([P, 1], F32, name=f"total{c}")
+            nc.scalar.activation(out=p[:], in_=scores[c][:], func=EXP, bias=negm[c][:], scale=1.0, accum_out=total[:])
+            sink_e = keep.tile([P, 1], F32, name=f"sink_e{c}")
+            nc.scalar.activation(out=sink_e[:], in_=sink_n[:, c : c + 1], func=EXP, bias=negm[c][:], scale=-1.0)
+            probs.append(p)
+            sums.append((total, sink_e))
+        for c in range(2):
+            p_ps = ps.tile([P, 4, P], F32, name="p_ps", tag="turn")
+            for t in range(4):
+                nc.tensor.transpose(p_ps[:, t, :], probs[c][:, t * P : (t + 1) * P], ident_f[:])
+            w_s = keep.tile([P, P, 4], BF16, name=f"w_s{c}", align_bytes=64)
+            nc.vector.tensor_tensor(
+                out=w_s[:],
+                in0=p_ps[:].rearrange("s t q -> s q t"),
+                in1=vs_c[:].unsqueeze(1).to_broadcast([P, P, 4]),
+                op=MULT,
+            )
+            wc = keep.tile([P, P], U32, name=f"wc{c}", align_bytes=64)
+            ws = keep.tile([P, P], U8, name=f"ws{c}", align_bytes=64)
+            nc.vector.quantize_mx(out=wc[:].bitcast(FP8X4), scales=ws[:], in_=w_s[:].rearrange("p q t -> p (q t)"))
+            y_ps = ps.tile([P, 2, P], F32, name="y_ps", tag="y")
+            for h in range(2):
+                rows = slice(h * P, (h + 1) * P)
+                nc.tensor.matmul_mx(
+                    out=y_ps[:, h, :],
+                    lhsT=v_codes[:, rows].bitcast(FP8X4),
+                    lhsT_scale=v_scales[:, rows],
+                    rhs=wc[:].bitcast(FP8X4),
+                    rhs_scale=ws[:],
+                    start=True,
+                    stop=True,
+                )
+            y_banks.append(y_ps)
+        for c in range(2):
+            total, sink_e = sums[c]
+            full = keep.tile([P, 1], F32, name=f"full{c}")
+            nc.vector.tensor_tensor(out=full[:], in0=total[:], in1=sink_e[:], op=ADD)
+            recip = keep.tile([P, 1], F32, name=f"recip{c}")
+            nc.vector.reciprocal(out=recip[:], in_=full[:])
+            r_ps = ps.tile([P, P], F32, name="r_ps", tag="recip")
+            nc.tensor.transpose(r_ps[:], recip[:].to_broadcast([P, P]), ident_f[:])
+            nc.scalar.activation(out=recip_b[c][:], in_=r_ps[:], func=COPY)
+        for c in range(2):
+            y = keep.tile([P, 2, P], F32, name=f"y{c}")
+            nc.scalar.activation(out=y[:], in_=y_banks[c][:], func=COPY)
+            for h in range(2):
+                nc.vector.tensor_tensor(
+                    placed[h][:].indirect(qoffs_t[:, c * 8 : (c + 1) * 8]), y[:, h, :], recip_b[c][:], MULT
+                )
+        out_rows = out.rearrange("(p h) n -> p h n", h=2)
+        for h in range(2):
+            nc.sync.dma_start(out=out_rows[:, h, :], in_=placed[h][:])

@@ -17,12 +17,10 @@ FP8X4 = mybir.dt.float8_e4m3fn_x4
 COPY = mybir.ActivationFunctionType.Copy
 EXP = mybir.ActivationFunctionType.Exp
 MULT = mybir.AluOpType.mult
+MIN = mybir.AluOpType.min
 ADD = mybir.AluOpType.add
-X = mybir.AxisListType.X
 
 K_SPLIT = 384
-V_SPLIT = T
-MIN = mybir.AluOpType.min
 
 
 def tile_attend_x_router_sink_kernel(tc, xq, kT, vT, vs, sink, offs, qoffs, out):
@@ -35,95 +33,91 @@ def tile_attend_x_router_sink_kernel(tc, xq, kT, vT, vs, sink, offs, qoffs, out)
         qoffs_t = keep.tile([P, NQ // 16], U16, name="qoffs_t")
         vs_raw = keep.tile([P, T], F32, name="vs_raw")
         k_raw = [keep.tile([P, 2, T], F32, name=f"k_raw{h}") for h in range(2)]
-        v_raw = keep.tile([P, 2, T], F32, name="v_raw")
+        v_raw = [keep.tile([P, T], F32, name=f"v_raw{h}") for h in range(2)]
         q_raw = [keep.tile([P, T], F32, name=f"q_raw{j}") for j in range(4)]
         k_rows = kT.rearrange("(p j) n -> p j n", j=4)
         q_rows = xq.rearrange("(p j) n -> p j n", j=4)
 
+        nc.sync.dma_start(out=v_raw[0][:], in_=vT[0 * P : (0 + 1) * P, :])
         nc.sync.dma_start(offs_t[:], offs)
-        nc.sync.dma_start(out=vs_raw[:], in_=vs)
-        for h in range(2):
-            nc.sync.dma_start(out=k_raw[h][:], in_=k_rows[:, 2 * h : 2 * h + 2, :])
+        nc.sync.dma_start(out=k_raw[0][:], in_=k_rows[:, 2 * 0 : 2 * 0 + 2, :])
+        nc.sync.dma_start(out=v_raw[1][:], in_=vT[1 * P : (1 + 1) * P, :])
         nc.sync.dma_start(qoffs_t[:], qoffs)
-        nc.sync.dma_start(out=v_raw[:], in_=vT.rearrange("(p h) n -> p h n", h=2))
-        for j in range(4):
-            nc.sync.dma_start(out=q_raw[j][:], in_=q_rows[:, j, :])
+        nc.sync.dma_start(out=k_raw[1][:], in_=k_rows[:, 2 * 1 : 2 * 1 + 2, :])
+        nc.sync.dma_start(out=q_raw[0][:], in_=q_rows[:, 0, :])
+        nc.sync.dma_start(out=q_raw[1][:], in_=q_rows[:, 1, :])
+        nc.sync.dma_start(out=q_raw[2][:], in_=q_rows[:, 2, :])
+        nc.sync.dma_start(out=q_raw[3][:], in_=q_rows[:, 3, :])
+        nc.sync.dma_start(out=vs_raw[:], in_=vs)
 
-        ident_f = keep.tile([P, P], F32, name="ident_f")
-        make_identity(nc, ident_f[:])
+        ident = keep.tile([P, P], F32, name="ident")
+        make_identity(nc, ident[:])
         sink_row = keep.tile([P, NQ], F32, name="sink_row")
         nc.gpsimd.memset(sink_row[:], 0.0)
         nc.scalar.dma_start(out=sink_row[0:1, :], in_=sink.rearrange("b q o -> b (q o)"))
-        ident_b = keep.tile([P, P], BF16, name="ident_b")
-        make_identity(nc, ident_b[:])
         placed = [keep.tile([P, T], F32, name=f"placed{h}") for h in range(2)]
         for h in range(2):
             nc.gpsimd.memset(placed[h][:], 0.0)
         dummy = keep.tile([P, 1], F32, name="dummy")
-        nc.scalar.activation(out=dummy[:], in_=ident_f[:, 0:1], func=EXP)
-
-        vs_g = keep.tile([P, N], F32, name="vs_g")
-        nc.vector.tensor_copy(vs_g[:], vs_raw[:].indirect(offs_t[:]))
-        vs_ps = ps.tile([P, 4, P], F32, name="vs_ps", tag="turn")
-        for t in range(4):
-            nc.tensor.transpose(vs_ps[:, t, :], vs_g[:, t::4], ident_f[:])
-        vs_c = keep.tile([P, 4], F32, name="vs_c")
-        nc.scalar.activation(out=vs_c[:], in_=vs_ps[:, :, 0], func=COPY)
-
+        nc.scalar.activation(out=dummy[:], in_=ident[:, 0:1], func=EXP)
         sink_ps = ps.tile([P, 2, P], F32, name="sink_ps", tag="y")
         for c in range(2):
-            nc.tensor.transpose(sink_ps[:, c, :], sink_row[:, c * P : (c + 1) * P], ident_f[:])
+            nc.tensor.transpose(sink_ps[:, c, :], sink_row[:, c * P : (c + 1) * P], ident[:])
         sink_n = keep.tile([P, 2], F32, name="sink_n")
         nc.scalar.activation(out=sink_n[:], in_=sink_ps[:, :, 0], func=COPY, scale=-1.0)
 
-        def cast_pairs(dst, raw, split):
-            nc.scalar.activation(out=dst[:, :split, :], in_=raw[:, :, :split].rearrange("p u n -> p n u"), func=COPY)
-            if split < T:
-                nc.vector.tensor_copy(out=dst[:, split:, :], in_=raw[:, :, split:].rearrange("p u n -> p n u"))
-
+        v_codes = [keep.tile([P, P], U32, name=f"v_codes{h}", align_bytes=64) for h in range(2)]
+        v_scales = [keep.tile([P, P], U8, name=f"v_scales{h}", align_bytes=64) for h in range(2)]
+        v_s = [keep.tile([P, P, 4], BF16, name=f"v_s{h}", align_bytes=64) for h in range(2)]
+        v_g = [keep.tile([P, N], F32, name=f"v_g{h}") for h in range(2)]
         k_g = keep.tile([P, N * 4], BF16, name="k_g", align_bytes=64)
         k_words = k_g[:].bitcast(U32).rearrange("p (t s u) -> p s t u", t=4, u=2)
-        for h in range(2):
-            k_pair = keep.tile([P, T, 2], BF16, name=f"k_pair{h}")
-            cast_pairs(k_pair, k_raw[h], K_SPLIT)
-            window = k_pair[:].rearrange("p n u -> p (n u)").bitcast(U32)
-            nc.vector.tensor_copy(k_words[:, :, :, h], window.indirect(offs_t[:]))
         k_codes = keep.tile([P, N], U32, name="k_codes", align_bytes=64)
         k_scales = keep.tile([P, N], U8, name="k_scales", align_bytes=64)
-        nc.vector.quantize_mx(out=k_codes[:].bitcast(FP8X4), scales=k_scales[:], in_=k_g[:])
-
-        v_pair = keep.tile([P, T, 2], BF16, name="v_pair")
-        cast_pairs(v_pair, v_raw, V_SPLIT)
-        v_g = keep.tile([P, N, 2], BF16, name="v_g")
-        v_words = v_g[:].rearrange("p n u -> p (n u)").bitcast(U32).rearrange("p (t s) -> p s t", t=4)
-        window = v_pair[:].rearrange("p n u -> p (n u)").bitcast(U32)
-        nc.vector.tensor_copy(v_words, window.indirect(offs_t[:]))
-        v_ps = ps.tile([P, 4, 2, P], BF16, name="v_ps", tag="turn")
-        for t in range(4):
-            for h in range(2):
-                nc.tensor.transpose(v_ps[:, t, h, :], v_g[:, t * P : (t + 1) * P, h], ident_b[:])
-        v_s = keep.tile([P, 2 * P, 4], BF16, name="v_s", align_bytes=64)
-        nc.scalar.copy(out=v_s[:], in_=v_ps[:].rearrange("s t h e -> s (h e) t"))
-        v_codes = keep.tile([P, DV], U32, name="v_codes", align_bytes=64)
-        v_scales = keep.tile([P, DV], U8, name="v_scales", align_bytes=64)
-        nc.vector.quantize_mx(out=v_codes[:].bitcast(FP8X4), scales=v_scales[:], in_=v_s[:].rearrange("p e t -> p (e t)"))
-
         q_g = keep.tile([P, NQ, 4], BF16, name="q_g", align_bytes=64)
-        for j in range(4):
-            nc.vector.tensor_copy(q_g[:, :, j], q_raw[j][:].indirect(qoffs_t[:]))
         q_codes = keep.tile([P, NQ], U32, name="q_codes", align_bytes=64)
         q_scales = keep.tile([P, NQ], U8, name="q_scales", align_bytes=64)
-        for c in range(2):
-            cols = slice(c * P, (c + 1) * P)
+        halves = [slice(c * P, (c + 1) * P) for c in range(2)]
+
+        def gather_values(h):
+            nc.vector.tensor_copy(v_g[h][:], v_raw[h][:].indirect(offs_t[:]))
+            v_ps = ps.tile([P, 4, P], F32, name="v_ps", tag="turn", bufs=3)
+            for t in range(4):
+                nc.tensor.transpose(v_ps[:, t, :], v_g[h][:, t::4], ident[:])
+            nc.scalar.activation(out=v_s[h][:], in_=v_ps[:].rearrange("s t e -> s e t"), func=COPY)
+
+        def quantise_values(h):
+            nc.vector.quantize_mx(
+                out=v_codes[h][:].bitcast(FP8X4), scales=v_scales[h][:], in_=v_s[h][:].rearrange("p e t -> p (e t)")
+            )
+
+        def gather_keys(h):
+            k_pair = keep.tile([P, T, 2], BF16, name=f"k_pair{h}")
+            raw = k_raw[h][:].rearrange("p u n -> p n u")
+            nc.scalar.activation(out=k_pair[:, :K_SPLIT, :], in_=raw[:, :K_SPLIT, :], func=COPY)
+            nc.vector.tensor_copy(out=k_pair[:, K_SPLIT:, :], in_=raw[:, K_SPLIT:, :])
+            window = k_pair[:].rearrange("p n u -> p (n u)").bitcast(U32)
+            nc.vector.tensor_copy(k_words[:, :, :, h], window.indirect(offs_t[:]))
+
+        def gather_queries(j):
+            nc.vector.tensor_copy(q_g[:, :, j], q_raw[j][:].indirect(qoffs_t[:]))
+
+        gather_values(0)
+        gather_keys(0)
+        gather_values(1)
+        quantise_values(0)
+        gather_keys(1)
+        gather_queries(0)
+        nc.vector.quantize_mx(out=k_codes[:].bitcast(FP8X4), scales=k_scales[:], in_=k_g[:])
+        for j in range(1, 4):
+            gather_queries(j)
+        for cols in halves:
             nc.vector.quantize_mx(
                 out=q_codes[:, cols].bitcast(FP8X4), scales=q_scales[:, cols], in_=q_g[:, cols, :].rearrange("p q j -> p (q j)")
             )
-
-        scores, probs, sums = [], [], []
-        recip_b = [keep.tile([P, P], F32, name=f"recip_b{c}") for c in range(2)]
-        for c in range(2):
-            cols = slice(c * P, (c + 1) * P)
-            sc = ps.tile([P, N], F32, name="sc", tag="score")
+        scores = []
+        for cols in halves:
+            sc = ps.tile([P, N], F32, name="sc", tag="score", bufs=2)
             nc.tensor.matmul_mx(
                 out=sc[:],
                 lhsT=q_codes[:, cols].bitcast(FP8X4),
@@ -134,7 +128,14 @@ def tile_attend_x_router_sink_kernel(tc, xq, kT, vT, vs, sink, offs, qoffs, out)
                 stop=True,
             )
             scores.append(sc)
-        negm, y_banks = [], []
+
+        vs_g = keep.tile([P, N], F32, name="vs_g")
+        nc.vector.tensor_copy(vs_g[:], vs_raw[:].indirect(offs_t[:]))
+        vs_ps = ps.tile([P, 4, P], F32, name="vs_ps", tag="turn", bufs=3)
+        for t in range(4):
+            nc.tensor.transpose(vs_ps[:, t, :], vs_g[:, t::4], ident[:])
+
+        negm, probs, totals = [], [], []
         for c in range(2):
             nm = keep.tile([P, 1], F32, name=f"negm{c}")
             flipped = keep.tile([P, N], F32, name=f"flipped{c}")
@@ -142,22 +143,41 @@ def tile_attend_x_router_sink_kernel(tc, xq, kT, vT, vs, sink, offs, qoffs, out)
                 out=flipped[:], in0=scores[c][:], scalar1=-1.0, scalar2=sink_n[:, c : c + 1], op0=MULT, op1=MIN, accum_out=nm[:]
             )
             negm.append(nm)
+        quantise_values(1)
         for c in range(2):
             p = keep.tile([P, N], F32, name=f"p{c}")
             total = keep.tile([P, 1], F32, name=f"total{c}")
             nc.scalar.activation(out=p[:], in_=scores[c][:], func=EXP, bias=negm[c][:], scale=1.0, accum_out=total[:])
+            probs.append(p)
+            totals.append(total)
+        vs_c = keep.tile([P, 4], F32, name="vs_c")
+        nc.scalar.activation(out=vs_c[:], in_=vs_ps[:, :, 0], func=COPY)
+        p_banks, recips = [], []
+        for c in range(2):
+            p_ps = ps.tile([P, 4, P], F32, name="p_ps", tag="turn", bufs=3)
+            for t in range(4):
+                nc.tensor.transpose(p_ps[:, t, :], probs[c][:, t * P : (t + 1) * P], ident[:])
+            p_banks.append(p_ps)
+        for c in range(2):
             sink_e = keep.tile([P, 1], F32, name=f"sink_e{c}")
             nc.scalar.activation(out=sink_e[:], in_=sink_n[:, c : c + 1], func=EXP, bias=negm[c][:], scale=-1.0)
-            probs.append(p)
-            sums.append((total, sink_e))
+            full = keep.tile([P, 1], F32, name=f"full{c}")
+            nc.vector.tensor_tensor(out=full[:], in0=totals[c][:], in1=sink_e[:], op=ADD)
+            recip = keep.tile([P, 1], F32, name=f"recip{c}")
+            nc.vector.reciprocal(out=recip[:], in_=full[:])
+            recips.append(recip)
+        r_ps = ps.tile([P, 2, P], F32, name="r_ps", tag="recip", bufs=1)
         for c in range(2):
-            p_ps = ps.tile([P, 4, P], F32, name="p_ps", tag="turn")
-            for t in range(4):
-                nc.tensor.transpose(p_ps[:, t, :], probs[c][:, t * P : (t + 1) * P], ident_f[:])
+            nc.tensor.transpose(r_ps[:, c, :], recips[c][:].to_broadcast([P, P]), ident[:])
+        recip_b = keep.tile([P, 2, P], F32, name="recip_b")
+        nc.scalar.activation(out=recip_b[:], in_=r_ps[:], func=COPY)
+
+        y_banks = []
+        for c in range(2):
             w_s = keep.tile([P, P, 4], BF16, name=f"w_s{c}", align_bytes=64)
             nc.vector.tensor_tensor(
                 out=w_s[:],
-                in0=p_ps[:].rearrange("s t q -> s q t"),
+                in0=p_banks[c][:].rearrange("s t q -> s q t"),
                 in1=vs_c[:].unsqueeze(1).to_broadcast([P, P, 4]),
                 op=MULT,
             )
@@ -166,11 +186,10 @@ def tile_attend_x_router_sink_kernel(tc, xq, kT, vT, vs, sink, offs, qoffs, out)
             nc.vector.quantize_mx(out=wc[:].bitcast(FP8X4), scales=ws[:], in_=w_s[:].rearrange("p q t -> p (q t)"))
             y_ps = ps.tile([P, 2, P], F32, name="y_ps", tag="y")
             for h in range(2):
-                rows = slice(h * P, (h + 1) * P)
                 nc.tensor.matmul_mx(
                     out=y_ps[:, h, :],
-                    lhsT=v_codes[:, rows].bitcast(FP8X4),
-                    lhsT_scale=v_scales[:, rows],
+                    lhsT=v_codes[h][:].bitcast(FP8X4),
+                    lhsT_scale=v_scales[h][:],
                     rhs=wc[:].bitcast(FP8X4),
                     rhs_scale=ws[:],
                     start=True,
@@ -178,21 +197,11 @@ def tile_attend_x_router_sink_kernel(tc, xq, kT, vT, vs, sink, offs, qoffs, out)
                 )
             y_banks.append(y_ps)
         for c in range(2):
-            total, sink_e = sums[c]
-            full = keep.tile([P, 1], F32, name=f"full{c}")
-            nc.vector.tensor_tensor(out=full[:], in0=total[:], in1=sink_e[:], op=ADD)
-            recip = keep.tile([P, 1], F32, name=f"recip{c}")
-            nc.vector.reciprocal(out=recip[:], in_=full[:])
-            r_ps = ps.tile([P, P], F32, name="r_ps", tag="recip")
-            nc.tensor.transpose(r_ps[:], recip[:].to_broadcast([P, P]), ident_f[:])
-            nc.scalar.activation(out=recip_b[c][:], in_=r_ps[:], func=COPY)
-        for c in range(2):
             y = keep.tile([P, 2, P], F32, name=f"y{c}")
             nc.scalar.activation(out=y[:], in_=y_banks[c][:], func=COPY)
             for h in range(2):
                 nc.vector.tensor_tensor(
-                    placed[h][:].indirect(qoffs_t[:, c * 8 : (c + 1) * 8]), y[:, h, :], recip_b[c][:], MULT
+                    placed[h][:].indirect(qoffs_t[:, c * 8 : (c + 1) * 8]), y[:, h, :], recip_b[:, c, :], MULT
                 )
-        out_rows = out.rearrange("(p h) n -> p h n", h=2)
         for h in range(2):
-            nc.sync.dma_start(out=out_rows[:, h, :], in_=placed[h][:])
+            nc.sync.dma_start(out=out[h * P : (h + 1) * P, :], in_=placed[h][:])

@@ -20,106 +20,119 @@ MULT = mybir.AluOpType.mult
 MIN = mybir.AluOpType.min
 ADD = mybir.AluOpType.add
 
-K_SPLIT = 384
+SCALAR_TOKENS = (384, 256)
 
 
 def tile_attend_x_router_sink_kernel(tc, xq, kT, vT, vs, sink, offs, qoffs, out):
     nc = tc.nc
     with ExitStack() as ctx:
         keep = ctx.enter_context(tc.tile_pool(name="keep", bufs=1))
-        ps = ctx.enter_context(tc.psum_pool(name="ps", bufs=2))
+        psum = ctx.enter_context(tc.psum_pool(name="psum", bufs=2))
+        tiles = [slice(c * P, (c + 1) * P) for c in range(2)]
 
         offs_t = keep.tile([P, N // 16], U16, name="offs_t")
         qoffs_t = keep.tile([P, NQ // 16], U16, name="qoffs_t")
-        vs_raw = keep.tile([P, T], F32, name="vs_raw")
-        k_raw = [keep.tile([P, 2, T], F32, name=f"k_raw{h}") for h in range(2)]
+        k_raw = [keep.tile([P, 2, T], F32, name=f"k_raw{u}", tag=f"k_raw{u}", align_bytes=64) for u in range(2)]
         v_raw = [keep.tile([P, T], F32, name=f"v_raw{h}") for h in range(2)]
         q_raw = [keep.tile([P, T], F32, name=f"q_raw{j}") for j in range(4)]
+        vs_raw = keep.tile([P, T], F32, name="vs_raw")
         k_rows = kT.rearrange("(p j) n -> p j n", j=4)
         q_rows = xq.rearrange("(p j) n -> p j n", j=4)
-
-        nc.sync.dma_start(out=v_raw[0][:], in_=vT[0 * P : (0 + 1) * P, :])
+        nc.sync.dma_start(out=k_raw[0][:], in_=k_rows[:, 0:2, :])
         nc.sync.dma_start(offs_t[:], offs)
-        nc.sync.dma_start(out=k_raw[0][:], in_=k_rows[:, 2 * 0 : 2 * 0 + 2, :])
-        nc.sync.dma_start(out=v_raw[1][:], in_=vT[1 * P : (1 + 1) * P, :])
+        nc.sync.dma_start(out=v_raw[0][:], in_=vT[tiles[0], :])
+        nc.sync.dma_start(out=k_raw[1][:], in_=k_rows[:, 2:4, :])
         nc.sync.dma_start(qoffs_t[:], qoffs)
-        nc.sync.dma_start(out=k_raw[1][:], in_=k_rows[:, 2 * 1 : 2 * 1 + 2, :])
-        nc.sync.dma_start(out=q_raw[0][:], in_=q_rows[:, 0, :])
-        nc.sync.dma_start(out=q_raw[1][:], in_=q_rows[:, 1, :])
-        nc.sync.dma_start(out=q_raw[2][:], in_=q_rows[:, 2, :])
-        nc.sync.dma_start(out=q_raw[3][:], in_=q_rows[:, 3, :])
+        for j in range(4):
+            nc.sync.dma_start(out=q_raw[j][:], in_=q_rows[:, j, :])
         nc.sync.dma_start(out=vs_raw[:], in_=vs)
+        nc.sync.dma_start(out=v_raw[1][:], in_=vT[tiles[1], :])
 
+        sink_row = keep.tile([P, NQ], F32, name="sink_row")
+        nc.vector.memset(sink_row[:], 0.0)
+        nc.scalar.dma_start(out=sink_row[0:1, :], in_=sink.rearrange("b q o -> b (q o)"))
         ident = keep.tile([P, P], F32, name="ident")
         make_identity(nc, ident[:])
-        sink_row = keep.tile([P, NQ], F32, name="sink_row")
-        nc.gpsimd.memset(sink_row[:], 0.0)
-        nc.scalar.dma_start(out=sink_row[0:1, :], in_=sink.rearrange("b q o -> b (q o)"))
+        ident_b = keep.tile([P, P], BF16, name="ident_b")
+        make_identity(nc, ident_b[:])
         placed = [keep.tile([P, T], F32, name=f"placed{h}") for h in range(2)]
         for h in range(2):
             nc.gpsimd.memset(placed[h][:], 0.0)
-        dummy = keep.tile([P, 1], F32, name="dummy")
-        nc.scalar.activation(out=dummy[:], in_=ident[:, 0:1], func=EXP)
-        sink_ps = ps.tile([P, 2, P], F32, name="sink_ps", tag="y")
-        for c in range(2):
-            nc.tensor.transpose(sink_ps[:, c, :], sink_row[:, c * P : (c + 1) * P], ident[:])
-        sink_n = keep.tile([P, 2], F32, name="sink_n")
-        nc.scalar.activation(out=sink_n[:], in_=sink_ps[:, :, 0], func=COPY, scale=-1.0)
+        table = keep.tile([P, 1], F32, name="table")
+        nc.scalar.activation(out=table[:], in_=ident[:, 0:1], func=EXP)
 
         v_codes = [keep.tile([P, P], U32, name=f"v_codes{h}", align_bytes=64) for h in range(2)]
         v_scales = [keep.tile([P, P], U8, name=f"v_scales{h}", align_bytes=64) for h in range(2)]
-        v_s = [keep.tile([P, P, 4], BF16, name=f"v_s{h}", align_bytes=64) for h in range(2)]
-        v_g = [keep.tile([P, N], F32, name=f"v_g{h}") for h in range(2)]
-        k_g = keep.tile([P, N * 4], BF16, name="k_g", align_bytes=64)
-        k_words = k_g[:].bitcast(U32).rearrange("p (t s u) -> p s t u", t=4, u=2)
-        k_codes = keep.tile([P, N], U32, name="k_codes", align_bytes=64)
-        k_scales = keep.tile([P, N], U8, name="k_scales", align_bytes=64)
-        q_g = keep.tile([P, NQ, 4], BF16, name="q_g", align_bytes=64)
-        q_codes = keep.tile([P, NQ], U32, name="q_codes", align_bytes=64)
-        q_scales = keep.tile([P, NQ], U8, name="q_scales", align_bytes=64)
-        halves = [slice(c * P, (c + 1) * P) for c in range(2)]
 
-        def gather_values(h):
-            nc.vector.tensor_copy(v_g[h][:], v_raw[h][:].indirect(offs_t[:]))
-            v_ps = ps.tile([P, 4, P], F32, name="v_ps", tag="turn", bufs=3)
+        def turn_values(v_g):
+            v_ps = psum.tile([P, 4, P], BF16, name="v_ps", tag="turn", bufs=3)
             for t in range(4):
-                nc.tensor.transpose(v_ps[:, t, :], v_g[h][:, t::4], ident[:])
-            nc.scalar.activation(out=v_s[h][:], in_=v_ps[:].rearrange("s t e -> s e t"), func=COPY)
+                nc.tensor.transpose(v_ps[:, t, :], v_g[:, t * P : (t + 1) * P], ident_b[:])
+            return v_ps
 
-        def quantise_values(h):
+        def interleave_values(h, v_ps):
+            v_s = keep.tile([P, P, 4], BF16, name=f"v_s{h}", align_bytes=64)
+            nc.scalar.copy(out=v_s[:], in_=v_ps[:].rearrange("s t e -> s e t"))
+            return v_s
+
+        def quantise_values(h, v_s):
             nc.vector.quantize_mx(
-                out=v_codes[h][:].bitcast(FP8X4), scales=v_scales[h][:], in_=v_s[h][:].rearrange("p e t -> p (e t)")
+                out=v_codes[h][:].bitcast(FP8X4), scales=v_scales[h][:], in_=v_s[:].rearrange("s e t -> s (e t)")
             )
 
-        def gather_keys(h):
-            k_pair = keep.tile([P, T, 2], BF16, name=f"k_pair{h}")
-            raw = k_raw[h][:].rearrange("p u n -> p n u")
-            nc.scalar.activation(out=k_pair[:, :K_SPLIT, :], in_=raw[:, :K_SPLIT, :], func=COPY)
-            nc.vector.tensor_copy(out=k_pair[:, K_SPLIT:, :], in_=raw[:, K_SPLIT:, :])
-            window = k_pair[:].rearrange("p n u -> p (n u)").bitcast(U32)
-            nc.vector.tensor_copy(k_words[:, :, :, h], window.indirect(offs_t[:]))
+        k_g = keep.tile([P, N * 4], BF16, name="k_g", align_bytes=64)
+        k_words = k_g[:].bitcast(U32).rearrange("p (t s u) -> p s t u", t=4, u=2)
 
-        def gather_queries(j):
-            nc.vector.tensor_copy(q_g[:, :, j], q_raw[j][:].indirect(qoffs_t[:]))
+        def gather_keys(u):
+            k_pair = keep.tile([P, T, 2], BF16, name=f"k_pair{u}", tag="step", align_bytes=64)
+            raw = k_raw[u][:].rearrange("p e n -> p n e")
+            split = SCALAR_TOKENS[u]
+            nc.scalar.activation(out=k_pair[:, :split, :], in_=raw[:, :split, :], func=COPY)
+            nc.vector.tensor_copy(out=k_pair[:, split:, :], in_=raw[:, split:, :])
+            window = k_pair[:].rearrange("p n e -> p (n e)").bitcast(U32)
+            nc.vector.tensor_copy(k_words[:, :, :, u], window.indirect(offs_t[:]))
 
-        gather_values(0)
         gather_keys(0)
-        gather_values(1)
-        quantise_values(0)
+        v_cast = keep.tile([P, T], BF16, name="v_cast")
+        nc.scalar.activation(out=v_cast[:], in_=v_raw[0][:], func=COPY)
+        v_g0 = keep.tile([P, N], BF16, name="v_g0")
+        nc.scalar.activation(
+            out=v_g0[:].rearrange("p (t s) -> p s t", t=4), in_=v_cast[:].indirect(offs_t[:]), func=COPY
+        )
+        v_ps0 = turn_values(v_g0)
         gather_keys(1)
-        gather_queries(0)
+
+        q_cast = keep.tile([P, 2, T], BF16, name="q_cast", tag="k_raw1", align_bytes=64)
+        for j in range(2):
+            nc.scalar.activation(out=q_cast[:, j, :], in_=q_raw[j][:], func=COPY)
+        q_g = keep.tile([P, NQ, 4], BF16, name="q_g", tag="step", align_bytes=64)
+        for j in range(2):
+            nc.scalar.activation(out=q_g[:, :, j], in_=q_cast[:, j, :].indirect(qoffs_t[:]), func=COPY)
+        k_codes = keep.tile([P, N], U32, name="k_codes", align_bytes=64)
+        k_scales = keep.tile([P, N], U8, name="k_scales", align_bytes=64)
         nc.vector.quantize_mx(out=k_codes[:].bitcast(FP8X4), scales=k_scales[:], in_=k_g[:])
-        for j in range(1, 4):
-            gather_queries(j)
-        for cols in halves:
+        nc.vector.tensor_copy(q_g[:, :, 2], q_raw[2][:].indirect(qoffs_t[:]))
+        v_s0 = interleave_values(0, v_ps0)
+        for c in range(2):
+            nc.vector.tensor_copy(q_g[:, tiles[c], 3], q_raw[3][:].indirect(qoffs_t[:, c * 8 : (c + 1) * 8]))
+        q_codes = keep.tile([P, NQ], U32, name="q_codes", align_bytes=64)
+        q_scales = keep.tile([P, NQ], U8, name="q_scales", align_bytes=64)
+        for cols in tiles:
             nc.vector.quantize_mx(
                 out=q_codes[:, cols].bitcast(FP8X4), scales=q_scales[:, cols], in_=q_g[:, cols, :].rearrange("p q j -> p (q j)")
             )
+
+        sink_ps = psum.tile([P, 2, P], F32, name="sink_ps", tag="y")
+        for c in range(2):
+            nc.tensor.transpose(sink_ps[:, c, :], sink_row[:, tiles[c]], ident[:])
+        sink_n = keep.tile([P, 2], F32, name="sink_n", tag="k_raw1", align_bytes=64)
+        nc.scalar.activation(out=sink_n[:], in_=sink_ps[:, :, 0], func=COPY, scale=-1.0)
+
         scores = []
-        for cols in halves:
-            sc = ps.tile([P, N], F32, name="sc", tag="score", bufs=2)
+        for cols in tiles:
+            score = psum.tile([P, N], F32, name="score", tag="score")
             nc.tensor.matmul_mx(
-                out=sc[:],
+                out=score[:],
                 lhsT=q_codes[:, cols].bitcast(FP8X4),
                 lhsT_scale=q_scales[:, cols],
                 rhs=k_codes[:].bitcast(FP8X4),
@@ -127,53 +140,67 @@ def tile_attend_x_router_sink_kernel(tc, xq, kT, vT, vs, sink, offs, qoffs, out)
                 start=True,
                 stop=True,
             )
-            scores.append(sc)
+            scores.append(score)
 
-        vs_g = keep.tile([P, N], F32, name="vs_g")
+        vs_g = keep.tile([P, N], F32, name="vs_g", tag="step", align_bytes=64)
         nc.vector.tensor_copy(vs_g[:], vs_raw[:].indirect(offs_t[:]))
-        vs_ps = ps.tile([P, 4, P], F32, name="vs_ps", tag="turn", bufs=3)
+        vs_ps = psum.tile([P, 4, P], F32, name="vs_ps", tag="turn", bufs=3)
         for t in range(4):
             nc.tensor.transpose(vs_ps[:, t, :], vs_g[:, t::4], ident[:])
 
-        negm, probs, totals = [], [], []
+        neg_max = []
         for c in range(2):
-            nm = keep.tile([P, 1], F32, name=f"negm{c}")
-            flipped = keep.tile([P, N], F32, name=f"flipped{c}")
+            least = keep.tile([P, 1], F32, name=f"neg_max{c}")
+            flipped = keep.tile([P, N], F32, name=f"flipped{c}", tag=f"flipped{c}", align_bytes=64)
             nc.vector.tensor_scalar(
-                out=flipped[:], in0=scores[c][:], scalar1=-1.0, scalar2=sink_n[:, c : c + 1], op0=MULT, op1=MIN, accum_out=nm[:]
+                out=flipped[:],
+                in0=scores[c][:],
+                scalar1=-1.0,
+                scalar2=sink_n[:, c : c + 1],
+                op0=MULT,
+                op1=MIN,
+                accum_out=least[:],
             )
-            negm.append(nm)
-        quantise_values(1)
+            neg_max.append(least)
+        vs_c = keep.tile([P, 4], F32, name="vs_c")
+        sums, p_banks = [], []
         for c in range(2):
             p = keep.tile([P, N], F32, name=f"p{c}")
-            total = keep.tile([P, 1], F32, name=f"total{c}")
-            nc.scalar.activation(out=p[:], in_=scores[c][:], func=EXP, bias=negm[c][:], scale=1.0, accum_out=total[:])
-            probs.append(p)
-            totals.append(total)
-        vs_c = keep.tile([P, 4], F32, name="vs_c")
-        nc.scalar.activation(out=vs_c[:], in_=vs_ps[:, :, 0], func=COPY)
-        p_banks, recips = [], []
-        for c in range(2):
-            p_ps = ps.tile([P, 4, P], F32, name="p_ps", tag="turn", bufs=3)
-            for t in range(4):
-                nc.tensor.transpose(p_ps[:, t, :], probs[c][:, t * P : (t + 1) * P], ident[:])
+            terms = keep.tile([P, 3], F32, name=f"terms{c}")
+            p_ps = psum.tile([P, 4, P], F32, name="p_ps", tag="turn", bufs=3)
+            for half in range(2):
+                cols = slice(half * 2 * P, (half + 1) * 2 * P)
+                nc.scalar.activation(
+                    out=p[:, cols],
+                    in_=scores[c][:, cols],
+                    func=EXP,
+                    bias=neg_max[c][:],
+                    scale=1.0,
+                    accum_out=terms[:, half : half + 1],
+                )
+                for t in (2 * half, 2 * half + 1):
+                    nc.tensor.transpose(p_ps[:, t, :], p[:, t * P : (t + 1) * P], ident[:])
+            nc.scalar.activation(
+                out=terms[:, 2:3], in_=sink_n[:, c : c + 1], func=EXP, bias=neg_max[c][:], scale=-1.0
+            )
+            if c == 0:
+                nc.scalar.activation(out=vs_c[:], in_=vs_ps[:, :, 0], func=COPY)
+            sums.append(terms)
             p_banks.append(p_ps)
-        for c in range(2):
-            sink_e = keep.tile([P, 1], F32, name=f"sink_e{c}")
-            nc.scalar.activation(out=sink_e[:], in_=sink_n[:, c : c + 1], func=EXP, bias=negm[c][:], scale=-1.0)
-            full = keep.tile([P, 1], F32, name=f"full{c}")
-            nc.vector.tensor_tensor(out=full[:], in0=totals[c][:], in1=sink_e[:], op=ADD)
-            recip = keep.tile([P, 1], F32, name=f"recip{c}")
-            nc.vector.reciprocal(out=recip[:], in_=full[:])
-            recips.append(recip)
-        r_ps = ps.tile([P, 2, P], F32, name="r_ps", tag="recip", bufs=1)
-        for c in range(2):
-            nc.tensor.transpose(r_ps[:, c, :], recips[c][:].to_broadcast([P, P]), ident[:])
-        recip_b = keep.tile([P, 2, P], F32, name="recip_b")
-        nc.scalar.activation(out=recip_b[:], in_=r_ps[:], func=COPY)
 
-        y_banks = []
+        v_g1 = keep.tile([P, N], BF16, name="v_g1", tag="flipped1", align_bytes=64)
+        nc.vector.tensor_copy(v_g1[:].rearrange("p (t s) -> p s t", t=4), v_raw[1][:].indirect(offs_t[:]))
+        quantise_values(0, v_s0)
+
+        w_codes, w_scales, recips = [], [], []
         for c in range(2):
+            listed = keep.tile([P, 1], F32, name=f"listed{c}")
+            nc.gpsimd.tensor_tensor(out=listed[:], in0=sums[c][:, 0:1], in1=sums[c][:, 1:2], op=ADD)
+            total = keep.tile([P, 1], F32, name=f"total{c}")
+            nc.gpsimd.tensor_tensor(out=total[:], in0=listed[:], in1=sums[c][:, 2:3], op=ADD)
+            recip = keep.tile([P, 1], F32, name=f"recip{c}")
+            nc.vector.reciprocal(out=recip[:], in_=total[:])
+            recips.append(recip)
             w_s = keep.tile([P, P, 4], BF16, name=f"w_s{c}", align_bytes=64)
             nc.vector.tensor_tensor(
                 out=w_s[:],
@@ -181,27 +208,39 @@ def tile_attend_x_router_sink_kernel(tc, xq, kT, vT, vs, sink, offs, qoffs, out)
                 in1=vs_c[:].unsqueeze(1).to_broadcast([P, P, 4]),
                 op=MULT,
             )
-            wc = keep.tile([P, P], U32, name=f"wc{c}", align_bytes=64)
-            ws = keep.tile([P, P], U8, name=f"ws{c}", align_bytes=64)
-            nc.vector.quantize_mx(out=wc[:].bitcast(FP8X4), scales=ws[:], in_=w_s[:].rearrange("p q t -> p (q t)"))
-            y_ps = ps.tile([P, 2, P], F32, name="y_ps", tag="y")
-            for h in range(2):
+            codes = keep.tile([P, P], U32, name=f"w_codes{c}", align_bytes=64)
+            scales = keep.tile([P, P], U8, name=f"w_scales{c}", align_bytes=64)
+            nc.vector.quantize_mx(out=codes[:].bitcast(FP8X4), scales=scales[:], in_=w_s[:].rearrange("s q t -> s (q t)"))
+            w_codes.append(codes)
+            w_scales.append(scales)
+
+        v_s1 = interleave_values(1, turn_values(v_g1))
+        r_ps = psum.tile([P, 2, P], F32, name="r_ps", tag="recip", bufs=1)
+        for c in range(2):
+            nc.tensor.transpose(r_ps[:, c, :], recips[c][:].to_broadcast([P, P]), ident[:])
+        recip_b = keep.tile([P, 2, P], F32, name="recip_b")
+        nc.scalar.activation(out=recip_b[:], in_=r_ps[:], func=COPY)
+
+        for h in range(2):
+            if h == 1:
+                quantise_values(1, v_s1)
+            y_banks = []
+            for c in range(2):
+                y_ps = psum.tile([P, P], F32, name="y_ps", tag=("y", "score")[h])
                 nc.tensor.matmul_mx(
-                    out=y_ps[:, h, :],
+                    out=y_ps[:],
                     lhsT=v_codes[h][:].bitcast(FP8X4),
                     lhsT_scale=v_scales[h][:],
-                    rhs=wc[:].bitcast(FP8X4),
-                    rhs_scale=ws[:],
+                    rhs=w_codes[c][:].bitcast(FP8X4),
+                    rhs_scale=w_scales[c][:],
                     start=True,
                     stop=True,
                 )
-            y_banks.append(y_ps)
-        for c in range(2):
-            y = keep.tile([P, 2, P], F32, name=f"y{c}")
-            nc.scalar.activation(out=y[:], in_=y_banks[c][:], func=COPY)
-            for h in range(2):
+                y_banks.append(y_ps)
+            for c in range(2):
+                y = keep.tile([P, P], F32, name=f"y{h}{c}")
+                nc.scalar.activation(out=y[:], in_=y_banks[c][:], func=COPY)
                 nc.vector.tensor_tensor(
-                    placed[h][:].indirect(qoffs_t[:, c * 8 : (c + 1) * 8]), y[:, h, :], recip_b[:, c, :], MULT
+                    placed[h][:].indirect(qoffs_t[:, c * 8 : (c + 1) * 8]), y[:], recip_b[:, c, :], MULT
                 )
-        for h in range(2):
-            nc.sync.dma_start(out=out[h * P : (h + 1) * P, :], in_=placed[h][:])
+            nc.sync.dma_start(out=out[tiles[h], :], in_=placed[h][:])

@@ -18,7 +18,6 @@ COPY = mybir.ActivationFunctionType.Copy
 EXP = mybir.ActivationFunctionType.Exp
 MULT = mybir.AluOpType.mult
 MIN = mybir.AluOpType.min
-ADD = mybir.AluOpType.add
 
 SCALAR_TOKENS = (384, 256)
 
@@ -61,9 +60,6 @@ def tile_attend_x_router_sink_kernel(tc, xq, kT, vT, vs, sink, offs, qoffs, out)
         table = keep.tile([P, 1], F32, name="table")
         nc.scalar.activation(out=table[:], in_=ident[:, 0:1], func=EXP)
 
-        v_codes = [keep.tile([P, P], U32, name=f"v_codes{h}", align_bytes=64) for h in range(2)]
-        v_scales = [keep.tile([P, P], U8, name=f"v_scales{h}", align_bytes=64) for h in range(2)]
-
         def turn_values(v_g):
             v_ps = psum.tile([P, 4, P], BF16, name="v_ps", tag="turn", bufs=3)
             for t in range(4):
@@ -75,10 +71,14 @@ def tile_attend_x_router_sink_kernel(tc, xq, kT, vT, vs, sink, offs, qoffs, out)
             nc.scalar.copy(out=v_s[:], in_=v_ps[:].rearrange("s t e -> s e t"))
             return v_s
 
+        v_codes, v_scales = [], []
+
         def quantise_values(h, v_s):
-            nc.vector.quantize_mx(
-                out=v_codes[h][:].bitcast(FP8X4), scales=v_scales[h][:], in_=v_s[:].rearrange("s e t -> s (e t)")
-            )
+            codes = keep.tile([P, P], U32, name=f"v_codes{h}", tag=("flipped0", "v_codes1")[h], align_bytes=64)
+            scales = keep.tile([P, P], U8, name=f"v_scales{h}", align_bytes=64)
+            nc.vector.quantize_mx(out=codes[:].bitcast(FP8X4), scales=scales[:], in_=v_s[:].rearrange("s e t -> s (e t)"))
+            v_codes.append(codes)
+            v_scales.append(scales)
 
         k_g = keep.tile([P, N * 4], BF16, name="k_g", align_bytes=64)
         k_words = k_g[:].bitcast(U32).rearrange("p (t s u) -> p s t u", t=4, u=2)
@@ -162,11 +162,10 @@ def tile_attend_x_router_sink_kernel(tc, xq, kT, vT, vs, sink, offs, qoffs, out)
                 accum_out=least[:],
             )
             neg_max.append(least)
-        vs_c = keep.tile([P, 4], F32, name="vs_c")
-        sums, p_banks = [], []
+        terms = keep.tile([P, 2, 3], F32, name="terms")
+        p_banks = []
         for c in range(2):
             p = keep.tile([P, N], F32, name=f"p{c}")
-            terms = keep.tile([P, 3], F32, name=f"terms{c}")
             p_ps = psum.tile([P, 4, P], F32, name="p_ps", tag="turn", bufs=3)
             for half in range(2):
                 cols = slice(half * 2 * P, (half + 1) * 2 * P)
@@ -176,31 +175,28 @@ def tile_attend_x_router_sink_kernel(tc, xq, kT, vT, vs, sink, offs, qoffs, out)
                     func=EXP,
                     bias=neg_max[c][:],
                     scale=1.0,
-                    accum_out=terms[:, half : half + 1],
+                    accum_out=terms[:, c, half : half + 1],
                 )
                 for t in (2 * half, 2 * half + 1):
                     nc.tensor.transpose(p_ps[:, t, :], p[:, t * P : (t + 1) * P], ident[:])
-            nc.scalar.activation(
-                out=terms[:, 2:3], in_=sink_n[:, c : c + 1], func=EXP, bias=neg_max[c][:], scale=-1.0
-            )
-            if c == 0:
-                nc.scalar.activation(out=vs_c[:], in_=vs_ps[:, :, 0], func=COPY)
-            sums.append(terms)
+                if half == 0:
+                    nc.scalar.activation(
+                        out=terms[:, c, 2:3], in_=sink_n[:, c : c + 1], func=EXP, bias=neg_max[c][:], scale=-1.0
+                    )
             p_banks.append(p_ps)
+        vs_c = keep.tile([P, 4], F32, name="vs_c")
+        nc.scalar.activation(out=vs_c[:], in_=vs_ps[:, :, 0], func=COPY)
 
         v_g1 = keep.tile([P, N], BF16, name="v_g1", tag="flipped1", align_bytes=64)
         nc.vector.tensor_copy(v_g1[:].rearrange("p (t s) -> p s t", t=4), v_raw[1][:].indirect(offs_t[:]))
         quantise_values(0, v_s0)
 
-        w_codes, w_scales, recips = [], [], []
+        totals = keep.tile([P, 2], F32, name="totals")
+        nc.vector.reduce_sum(out=totals[:], in_=terms[:], axis=mybir.AxisListType.X)
+        recips = keep.tile([P, 2], F32, name="recips")
+        nc.vector.reciprocal(out=recips[:], in_=totals[:])
+        w_codes, w_scales = [], []
         for c in range(2):
-            listed = keep.tile([P, 1], F32, name=f"listed{c}")
-            nc.gpsimd.tensor_tensor(out=listed[:], in0=sums[c][:, 0:1], in1=sums[c][:, 1:2], op=ADD)
-            total = keep.tile([P, 1], F32, name=f"total{c}")
-            nc.gpsimd.tensor_tensor(out=total[:], in0=listed[:], in1=sums[c][:, 2:3], op=ADD)
-            recip = keep.tile([P, 1], F32, name=f"recip{c}")
-            nc.vector.reciprocal(out=recip[:], in_=total[:])
-            recips.append(recip)
             w_s = keep.tile([P, P, 4], BF16, name=f"w_s{c}", align_bytes=64)
             nc.vector.tensor_tensor(
                 out=w_s[:],
@@ -217,7 +213,7 @@ def tile_attend_x_router_sink_kernel(tc, xq, kT, vT, vs, sink, offs, qoffs, out)
         v_s1 = interleave_values(1, turn_values(v_g1))
         r_ps = psum.tile([P, 2, P], F32, name="r_ps", tag="recip", bufs=1)
         for c in range(2):
-            nc.tensor.transpose(r_ps[:, c, :], recips[c][:].to_broadcast([P, P]), ident[:])
+            nc.tensor.transpose(r_ps[:, c, :], recips[:, c : c + 1].to_broadcast([P, P]), ident[:])
         recip_b = keep.tile([P, 2, P], F32, name="recip_b")
         nc.scalar.activation(out=recip_b[:], in_=r_ps[:], func=COPY)
 

from contextlib import ExitStack

import concourse.mybir as mybir
from concourse.masks import make_identity

D, T, N, NQ, DV = 512, 1024, 512, 256, 256
P = 128
FLOPS = 2 * NQ * N * D + 2 * NQ * N * DV

F32 = mybir.dt.float32
BF16 = mybir.dt.bfloat16
U32 = mybir.dt.uint32
U16 = mybir.dt.uint16
U8 = mybir.dt.uint8
FP8X4 = mybir.dt.float8_e4m3fn_x4

COPY = mybir.ActivationFunctionType.Copy
EXP = mybir.ActivationFunctionType.Exp
MULT = mybir.AluOpType.mult
MIN = mybir.AluOpType.min

SCALAR_TOKENS = (384, 256)


def tile_attend_x_router_sink_kernel(tc, xq, kT, vT, vs, sink, offs, qoffs, out):
    nc = tc.nc
    with ExitStack() as ctx:
        keep = ctx.enter_context(tc.tile_pool(name="keep", bufs=1))
        psum = ctx.enter_context(tc.psum_pool(name="psum", bufs=2))
        tiles = [slice(c * P, (c + 1) * P) for c in range(2)]

        offs_t = keep.tile([P, N // 16], U16, name="offs_t")
        qoffs_t = keep.tile([P, NQ // 16], U16, name="qoffs_t")
        k_raw = [keep.tile([P, 2, T], F32, name=f"k_raw{u}", tag=f"k_raw{u}", align_bytes=64) for u in range(2)]
        v_raw = [keep.tile([P, T], F32, name=f"v_raw{h}") for h in range(2)]
        q_raw = [keep.tile([P, T], F32, name=f"q_raw{j}") for j in range(4)]
        vs_raw = keep.tile([P, T], F32, name="vs_raw")
        k_rows = kT.rearrange("(p j) n -> p j n", j=4)
        q_rows = xq.rearrange("(p j) n -> p j n", j=4)
        nc.sync.dma_start(out=k_raw[0][:], in_=k_rows[:, 0:2, :])
        nc.sync.dma_start(offs_t[:], offs)
        nc.sync.dma_start(out=v_raw[0][:], in_=vT[tiles[0], :])
        nc.sync.dma_start(out=k_raw[1][:], in_=k_rows[:, 2:4, :])
        nc.sync.dma_start(qoffs_t[:], qoffs)
        for j in range(4):
            nc.sync.dma_start(out=q_raw[j][:], in_=q_rows[:, j, :])
        nc.sync.dma_start(out=vs_raw[:], in_=vs)
        nc.sync.dma_start(out=v_raw[1][:], in_=vT[tiles[1], :])

        sink_row = keep.tile([P, NQ], F32, name="sink_row")
        nc.vector.memset(sink_row[:], 0.0)
        nc.scalar.dma_start(out=sink_row[0:1, :], in_=sink.rearrange("b q o -> b (q o)"))
        ident = keep.tile([P, P], F32, name="ident")
        make_identity(nc, ident[:])
        ident_b = keep.tile([P, P], BF16, name="ident_b")
        make_identity(nc, ident_b[:])
        placed = [keep.tile([P, T], F32, name=f"placed{h}") for h in range(2)]
        for h in range(2):
            nc.gpsimd.memset(placed[h][:], 0.0)
        table = keep.tile([P, 1], F32, name="table")
        nc.scalar.activation(out=table[:], in_=ident[:, 0:1], func=EXP)

        def turn_values(v_g):
            v_ps = psum.tile([P, 4, P], BF16, name="v_ps", tag="turn", bufs=3)
            for t in range(4):
                nc.tensor.transpose(v_ps[:, t, :], v_g[:, t * P : (t + 1) * P], ident_b[:])
            return v_ps

        def interleave_values(h, v_ps):
            v_s = keep.tile([P, P, 4], BF16, name=f"v_s{h}", align_bytes=64)
            nc.scalar.copy(out=v_s[:], in_=v_ps[:].rearrange("s t e -> s e t"))
            return v_s

        v_codes, v_scales = [], []

        def quantise_values(h, v_s):
            codes = keep.tile([P, P], U32, name=f"v_codes{h}", tag=("flipped0", "v_codes1")[h], align_bytes=64)
            scales = keep.tile([P, P], U8, name=f"v_scales{h}", align_bytes=64)
            nc.vector.quantize_mx(out=codes[:].bitcast(FP8X4), scales=scales[:], in_=v_s[:].rearrange("s e t -> s (e t)"))
            v_codes.append(codes)
            v_scales.append(scales)

        k_g = keep.tile([P, N * 4], BF16, name="k_g", align_bytes=64)
        k_words = k_g[:].bitcast(U32).rearrange("p (t s u) -> p s t u", t=4, u=2)

        def gather_keys(u):
            k_pair = keep.tile([P, T, 2], BF16, name=f"k_pair{u}", tag="step", align_bytes=64)
            raw = k_raw[u][:].rearrange("p e n -> p n e")
            split = SCALAR_TOKENS[u]
            nc.scalar.activation(out=k_pair[:, :split, :], in_=raw[:, :split, :], func=COPY)
            nc.vector.tensor_copy(out=k_pair[:, split:, :], in_=raw[:, split:, :])
            window = k_pair[:].rearrange("p n e -> p (n e)").bitcast(U32)
            nc.vector.tensor_copy(k_words[:, :, :, u], window.indirect(offs_t[:]))

        gather_keys(0)
        v_cast = keep.tile([P, T], BF16, name="v_cast")
        nc.scalar.activation(out=v_cast[:], in_=v_raw[0][:], func=COPY)
        v_g0 = keep.tile([P, N], BF16, name="v_g0")
        nc.scalar.activation(
            out=v_g0[:].rearrange("p (t s) -> p s t", t=4), in_=v_cast[:].indirect(offs_t[:]), func=COPY
        )
        v_ps0 = turn_values(v_g0)
        gather_keys(1)

        q_cast = keep.tile([P, 2, T], BF16, name="q_cast", tag="k_raw1", align_bytes=64)
        for j in range(2):
            nc.scalar.activation(out=q_cast[:, j, :], in_=q_raw[j][:], func=COPY)
        q_g = keep.tile([P, NQ, 4], BF16, name="q_g", tag="step", align_bytes=64)
        for j in range(2):
            nc.scalar.activation(out=q_g[:, :, j], in_=q_cast[:, j, :].indirect(qoffs_t[:]), func=COPY)
        k_codes = keep.tile([P, N], U32, name="k_codes", align_bytes=64)
        k_scales = keep.tile([P, N], U8, name="k_scales", align_bytes=64)
        nc.vector.quantize_mx(out=k_codes[:].bitcast(FP8X4), scales=k_scales[:], in_=k_g[:])
        nc.vector.tensor_copy(q_g[:, :, 2], q_raw[2][:].indirect(qoffs_t[:]))
        v_s0 = interleave_values(0, v_ps0)
        for c in range(2):
            nc.vector.tensor_copy(q_g[:, tiles[c], 3], q_raw[3][:].indirect(qoffs_t[:, c * 8 : (c + 1) * 8]))
        q_codes = keep.tile([P, NQ], U32, name="q_codes", align_bytes=64)
        q_scales = keep.tile([P, NQ], U8, name="q_scales", align_bytes=64)
        for cols in tiles:
            nc.vector.quantize_mx(
                out=q_codes[:, cols].bitcast(FP8X4), scales=q_scales[:, cols], in_=q_g[:, cols, :].rearrange("p q j -> p (q j)")
            )

        sink_ps = psum.tile([P, 2, P], F32, name="sink_ps", tag="y")
        for c in range(2):
            nc.tensor.transpose(sink_ps[:, c, :], sink_row[:, tiles[c]], ident[:])
        sink_n = keep.tile([P, 2], F32, name="sink_n", tag="k_raw1", align_bytes=64)
        nc.scalar.activation(out=sink_n[:], in_=sink_ps[:, :, 0], func=COPY, scale=-1.0)

        scores = []
        for cols in tiles:
            score = psum.tile([P, N], F32, name="score", tag="score")
            nc.tensor.matmul_mx(
                out=score[:],
                lhsT=q_codes[:, cols].bitcast(FP8X4),
                lhsT_scale=q_scales[:, cols],
                rhs=k_codes[:].bitcast(FP8X4),
                rhs_scale=k_scales[:],
                start=True,
                stop=True,
            )
            scores.append(score)

        vs_g = keep.tile([P, N], F32, name="vs_g", tag="step", align_bytes=64)
        nc.vector.tensor_copy(vs_g[:], vs_raw[:].indirect(offs_t[:]))
        vs_ps = psum.tile([P, 4, P], F32, name="vs_ps", tag="turn", bufs=3)
        for t in range(4):
            nc.tensor.transpose(vs_ps[:, t, :], vs_g[:, t::4], ident[:])

        neg_max = []
        for c in range(2):
            least = keep.tile([P, 1], F32, name=f"neg_max{c}")
            flipped = keep.tile([P, N], F32, name=f"flipped{c}", tag=f"flipped{c}", align_bytes=64)
            nc.vector.tensor_scalar(
                out=flipped[:],
                in0=scores[c][:],
                scalar1=-1.0,
                scalar2=sink_n[:, c : c + 1],
                op0=MULT,
                op1=MIN,
                accum_out=least[:],
            )
            neg_max.append(least)
        terms = keep.tile([P, 2, 3], F32, name="terms")
        p_banks = []
        for c in range(2):
            p = keep.tile([P, N], F32, name=f"p{c}")
            p_ps = psum.tile([P, 4, P], F32, name="p_ps", tag="turn", bufs=3)
            for half in range(2):
                cols = slice(half * 2 * P, (half + 1) * 2 * P)
                nc.scalar.activation(
                    out=p[:, cols],
                    in_=scores[c][:, cols],
                    func=EXP,
                    bias=neg_max[c][:],
                    scale=1.0,
                    accum_out=terms[:, c, half : half + 1],
                )
                for t in (2 * half, 2 * half + 1):
                    nc.tensor.transpose(p_ps[:, t, :], p[:, t * P : (t + 1) * P], ident[:])
                if half == 0:
                    nc.scalar.activation(
                        out=terms[:, c, 2:3], in_=sink_n[:, c : c + 1], func=EXP, bias=neg_max[c][:], scale=-1.0
                    )
            p_banks.append(p_ps)
        vs_c = keep.tile([P, 4], F32, name="vs_c")
        nc.scalar.activation(out=vs_c[:], in_=vs_ps[:, :, 0], func=COPY)

        v_g1 = keep.tile([P, N], BF16, name="v_g1", tag="flipped1", align_bytes=64)
        nc.vector.tensor_copy(v_g1[:].rearrange("p (t s) -> p s t", t=4), v_raw[1][:].indirect(offs_t[:]))
        quantise_values(0, v_s0)

        totals = keep.tile([P, 2], F32, name="totals")
        nc.vector.reduce_sum(out=totals[:], in_=terms[:], axis=mybir.AxisListType.X)
        recips = keep.tile([P, 2], F32, name="recips")
        nc.vector.reciprocal(out=recips[:], in_=totals[:])
        w_codes, w_scales = [], []
        for c in range(2):
            w_s = keep.tile([P, P, 4], BF16, name=f"w_s{c}", align_bytes=64)
            nc.vector.tensor_tensor(
                out=w_s[:],
                in0=p_banks[c][:].rearrange("s t q -> s q t"),
                in1=vs_c[:].unsqueeze(1).to_broadcast([P, P, 4]),
                op=MULT,
            )
            codes = keep.tile([P, P], U32, name=f"w_codes{c}", align_bytes=64)
            scales = keep.tile([P, P], U8, name=f"w_scales{c}", align_bytes=64)
            nc.vector.quantize_mx(out=codes[:].bitcast(FP8X4), scales=scales[:], in_=w_s[:].rearrange("s q t -> s (q t)"))
            w_codes.append(codes)
            w_scales.append(scales)

        v_s1 = interleave_values(1, turn_values(v_g1))
        r_ps = psum.tile([P, 2, P], F32, name="r_ps", tag="recip", bufs=1)
        for c in range(2):
            nc.tensor.transpose(r_ps[:, c, :], recips[:, c : c + 1].to_broadcast([P, P]), ident[:])
        recip_b = keep.tile([P, 2, P], F32, name="recip_b")
        nc.scalar.activation(out=recip_b[:], in_=r_ps[:], func=COPY)

        for h in range(2):
            if h == 1:
                quantise_values(1, v_s1)
            y_banks = []
            for c in range(2):
                y_ps = psum.tile([P, P], F32, name="y_ps", tag=("y", "score")[h])
                nc.tensor.matmul_mx(
                    out=y_ps[:],
                    lhsT=v_codes[h][:].bitcast(FP8X4),
                    lhsT_scale=v_scales[h][:],
                    rhs=w_codes[c][:].bitcast(FP8X4),
                    rhs_scale=w_scales[c][:],
                    start=True,
                    stop=True,
                )
                y_banks.append(y_ps)
            for c in range(2):
                y = keep.tile([P, P], F32, name=f"y{h}{c}")
                nc.scalar.activation(out=y[:], in_=y_banks[c][:], func=COPY)
                nc.vector.tensor_tensor(
                    placed[h][:].indirect(qoffs_t[:, c * 8 : (c + 1) * 8]), y[:], recip_b[:, c, :], MULT
                )
            nc.sync.dma_start(out=out[tiles[h], :], in_=placed[h][:])
